import numpy as np
import ml_dtypes


def mxq(x, axis, fmt="e4m3"):
    dtype, down = {"e4m3": (ml_dtypes.float8_e4m3fn, 7), "e5m2": (ml_dtypes.float8_e5m2, 14)}[fmt]
    v = np.moveaxis(np.asarray(x, np.float32).astype(ml_dtypes.bfloat16).astype(np.float64), axis, -1)
    blocks = v.reshape(v.shape[:-1] + (-1, 32))
    amax = np.abs(blocks).max(-1, keepdims=True)
    byte = np.maximum(np.where(amax > 0, np.frexp(amax)[1] - 1 + 127, 0) - down, 1)
    scale = np.exp2(byte - 127.0)
    codes = (blocks / scale).astype(np.float32).astype(dtype).astype(np.float64)
    return np.moveaxis((codes * scale).reshape(v.shape), -1, axis)


WIDE = False


def mx_kscale(k, group=512):
    if not WIDE:
        return np.ones(k)
    levels = np.array([10, -10, 5, -5, 0])
    if group != 512:
        return np.exp2(np.random.permutation(np.resize(levels, k // group))).repeat(group)
    if k % 512:
        return np.exp2(np.random.permutation(np.resize(levels, k // 32))).repeat(32)
    a = np.empty((k // 512, 16))
    for p in range(k // 512):
        a[p, :8] = np.random.permutation(np.resize(levels, 8))
        for g in range(8):
            far = levels[np.abs(levels - a[p, g]) >= 10]
            a[p, g + 8] = far[np.random.randint(len(far))]
    return np.exp2(a.ravel()).repeat(32)


def f64(x):
    return np.asarray(x).astype(np.float64)


def striped(idx):
    return np.tile(np.asarray(idx).reshape(-1, 16).T, (8, 1)).astype(np.uint16)


def unstriped(offs):
    return offs[:16].T.reshape(-1).astype(np.int64)


H, KV, D, NQ, N = 2, 2, 256, 512, 512


def setup_inputs():
    n = np.random.standard_normal
    s = mx_kscale(D, 0)[:, None]
    u = mx_kscale(N)
    t = np.random.uniform(0.5, 2.0, N) * u
    v = n((KV, N, 128))
    return {
        "qT": (n((H, D, NQ)) * s * (0.70 / np.sqrt(D))).astype(np.float32),
        "kT": (n((KV, D, N)) / s).astype(np.float32),
        "t": t.reshape(N, 1).astype(np.float32),
        "v": (v / t[:, None]).astype(np.float32),
        "mask": (np.arange(N)[:, None] <= np.sort(np.random.randint(N // 4, N, NQ))[None, :]).astype(np.float32),
        "gn": np.tile(np.random.uniform(0.5, 2.0, 128), (128, 1)).astype(np.float32),
    }


def reference(qT, kT, t, v, mask, gn):
    a = mxq(f64(kT), 1, "e4m3").transpose(0, 2, 1) @ mxq(f64(qT), 1, "e4m3")
    p = a / (1.0 + np.exp(-a))
    p = p * f64(mask)
    w = p * f64(t)
    y = mxq(w, 1, "e4m3").transpose(0, 2, 1) @ mxq(f64(v), 1, "e4m3")
    y = y / 16.0
    y = y / np.sqrt(np.mean(np.square(y), -1, keepdims=True) + 1e-5) * f64(gn)[:1]
    return y

@@ -1,0 +1,248 @@
+from contextlib import ExitStack
+
+import concourse.mybir as mybir
+
+H, D, NQ, N, E = 2, 256, 512, 512, 128
+FLOPS = 2 * H * N * NQ * (D + E)
+
+F32 = mybir.dt.float32
+BF16 = mybir.dt.bfloat16
+U32 = mybir.dt.uint32
+U8 = mybir.dt.uint8
+FP8X4 = mybir.dt.float8_e4m3fn_x4
+ACT = mybir.ActivationFunctionType
+MULT = mybir.AluOpType.mult
+
+P = 128
+PACK = 4
+ROWS = D // PACK
+QC = 128
+CHUNKS = NQ // QC
+HALF = NQ // 2
+RUN = 4
+K_SPLIT = 84
+UNITS = CHUNKS * H
+Y_BANK = [(0, 0), (0, 1), (0, 2), (0, 3), (1, 0), (1, 1), (2, 0), (3, 0)]
+EPS = 1e-5
+
+
+def tile_rows_a_silu_mask_onorm_kernel(tc, qT, kT, t, v, mask, gn, out):
+    nc = tc.nc
+    with ExitStack() as ctx:
+        sb = ctx.enter_context(tc.tile_pool(name="sb", bufs=1))
+        ps = ctx.enter_context(tc.psum_pool(name="ps", bufs=1))
+        ctx.enter_context(tc.manual_schedule())
+
+        def sbuf(name, shape, dtype):
+            return sb.tile(shape, dtype, name=name, align_bytes=64)
+
+        k_raw = sbuf("k_raw", [P, PACK, N], F32)
+        q_raw = [sbuf("q_raw%d" % a, [P, PACK, HALF], F32) for a in range(2)]
+        m_raw = [sbuf("m_raw%d" % a, [P, PACK, HALF], F32) for a in range(2)]
+        t_sb = sbuf("t_sb", [P, PACK], F32)
+        v_raw = sbuf("v_raw", [P, H, PACK, E], F32)
+        gn_sb = sbuf("gn_sb", [P, E], F32)
+
+        q_view = qT.rearrange("h (p j) q -> (h p) j q", j=PACK)
+        m_view = mask.rearrange("(p r) q -> p r q", r=PACK)
+        nc.sync.dma_start(out=k_raw[:], in_=kT.rearrange("h (p j) n -> (h p) j n", j=PACK))
+        nc.sync.dma_start(out=q_raw[0][:], in_=q_view[:, :, 0:HALF])
+        nc.sync.dma_start(out=t_sb[:], in_=t.rearrange("(p r) o -> p (r o)", r=PACK))
+        nc.sync.dma_start(out=m_raw[0][:], in_=m_view[:, :, 0:HALF])
+        nc.sync.dma_start(out=q_raw[1][:], in_=q_view[:, :, HALF:NQ])
+        nc.sync.dma_start(out=m_raw[1][:], in_=m_view[:, :, HALF:NQ])
+        nc.sync.dma_start(out=v_raw[:], in_=v.rearrange("h (p r) e -> p h r e", r=PACK))
+        nc.sync.dma_start(out=gn_sb[:], in_=gn)
+
+        k_bf = sbuf("k_bf", [P, PACK, P, PACK], BF16)
+        k_codes = sbuf("k_codes", [P, PACK, P], U32)
+        k_scales = sbuf("k_scales", [P, PACK, P], U8)
+        q_bf = [sbuf("q_bf%d" % c, [P, QC, PACK], BF16) for c in range(CHUNKS)]
+        q_codes = [sbuf("q_codes%d" % c, [P, QC], U32) for c in range(CHUNKS)]
+        q_scales = [sbuf("q_scales%d" % c, [P, QC], U8) for c in range(CHUNKS)]
+        v_bf = sbuf("v_bf", [P, H, E, PACK], BF16)
+        v_codes = sbuf("v_codes", [P, H, E], U32)
+        v_scales = sbuf("v_scales", [P, H, E], U8)
+        mt = [sbuf("mt%d" % a, [P, PACK, HALF], F32) for a in range(2)]
+        silu = [sbuf("silu%d" % u, [P, PACK * QC], F32) for u in range(UNITS)]
+        w_bf = [sbuf("w_bf%d" % u, [P, QC, PACK], BF16) for u in range(UNITS)]
+        w_codes = [sbuf("w_codes%d" % u, [P, QC], U32) for u in range(UNITS)]
+        w_scales = [sbuf("w_scales%d" % u, [P, QC], U8) for u in range(UNITS)]
+        squares = [sbuf("squares%d" % u, [P, E], BF16) for u in range(UNITS)]
+        sums = sbuf("sums", [P, UNITS], F32)
+        rinv = sbuf("rinv", [P, UNITS], F32)
+        res = [sbuf("res%d" % u, [P, E], F32) for u in range(UNITS)]
+        s_banks = [[ps.tile([P, PACK, QC], F32, name="s%d_%d" % (h, b)) for b in range(2)] for h in range(H)]
+        y_banks = [ps.tile([P, PACK, E], F32, name="y%d" % b) for b in range(4)]
+
+        def quantize(codes, scales, src):
+            nc.vector.quantize_mx(out=codes.bitcast(FP8X4), scales=scales, in_=src)
+
+        def copy_k(copy, s0, s1):
+            copy(
+                out=k_bf[:, :, s0:s1, :].rearrange("p r s j -> p s j r"),
+                in_=k_raw[:, :, PACK * s0 : PACK * s1].rearrange("p j (s r) -> p s j r", r=PACK),
+            )
+
+        def quant_k(r):
+            quantize(k_codes[:, r, :], k_scales[:, r, :], k_bf[:, r, :, :].rearrange("p s j -> p (s j)"))
+
+        def half_cols(c):
+            return c // 2, slice((c % 2) * QC, (c % 2 + 1) * QC)
+
+        def copy_q(copy, c):
+            a, cols = half_cols(c)
+            copy(
+                out=q_bf[c][:].rearrange("p (c i) j -> p c j i", i=RUN),
+                in_=q_raw[a][:, :, cols].rearrange("p j (c i) -> p c j i", i=RUN),
+            )
+
+        def quant_q(c):
+            quantize(q_codes[c][:], q_scales[c][:], q_bf[c][:].rearrange("p q j -> p (q j)"))
+
+        def copy_v():
+            nc.vector.tensor_copy(
+                out=v_bf[:].rearrange("p h (c i) r -> p h c r i", i=RUN),
+                in_=v_raw[:].rearrange("p h r (c i) -> p h c r i", i=RUN),
+            )
+
+        def quant_v():
+            quantize(
+                v_codes[:].rearrange("p h e -> p (h e)"),
+                v_scales[:].rearrange("p h e -> p (h e)"),
+                v_bf[:].rearrange("p h e r -> p (h e r)"),
+            )
+
+        def make_mt(a, r0, r1):
+            for r in range(r0, r1):
+                nc.vector.tensor_scalar(
+                    out=mt[a][:, r, :], in0=m_raw[a][:, r, :], scalar1=t_sb[:, r : r + 1], scalar2=None, op0=MULT
+                )
+
+        def scores(c):
+            for h in range(H):
+                for r in range(PACK):
+                    rows = slice(h * ROWS, (h + 1) * ROWS)
+                    nc.tensor.matmul_mx(
+                        out=s_banks[h][c % 2][:, r, :],
+                        lhsT=k_codes[rows, r, :].bitcast(FP8X4),
+                        lhsT_scale=k_scales[rows, r, :],
+                        rhs=q_codes[c][rows, :].bitcast(FP8X4),
+                        rhs_scale=q_scales[c][rows, :],
+                        start=True,
+                        stop=True,
+                    )
+
+        def act_silu(u):
+            c, h = divmod(u, H)
+            nc.scalar.activation(
+                out=silu[u][:].rearrange("p (c r i) -> p c r i", r=PACK, i=RUN),
+                in_=s_banks[h][c % 2][:].rearrange("p r (c i) -> p c r i", i=RUN),
+                func=ACT.Silu,
+            )
+
+        def weigh(u):
+            a, cols = half_cols(u // H)
+            nc.vector.tensor_tensor(
+                out=w_bf[u][:].rearrange("p (c i) r -> p c r i", i=RUN),
+                in0=silu[u][:].rearrange("p (c r i) -> p c r i", r=PACK, i=RUN),
+                in1=mt[a][:, :, cols].rearrange("p r (c i) -> p c r i", i=RUN),
+                op=MULT,
+            )
+
+        def quant_w(u):
+            quantize(w_codes[u][:], w_scales[u][:], w_bf[u][:].rearrange("p q r -> p (q r)"))
+
+        def y_of(u):
+            b, s = Y_BANK[u]
+            return y_banks[b][:, s, :]
+
+        def values(u):
+            h = u % H
+            nc.tensor.matmul_mx(
+                out=y_of(u),
+                lhsT=w_codes[u][:].bitcast(FP8X4),
+                lhsT_scale=w_scales[u][:],
+                rhs=v_codes[:, h, :].bitcast(FP8X4),
+                rhs_scale=v_scales[:, h, :],
+                start=True,
+                stop=True,
+            )
+
+        def square(u):
+            nc.scalar.activation(out=squares[u][:], in_=y_of(u), func=ACT.Square, accum_out=sums[:, u : u + 1])
+
+        def root(u0, u1):
+            nc.scalar.activation(
+                out=rinv[:, u0:u1], in_=sums[:, u0:u1], func=ACT.Abs_reciprocal_sqrt, scale=1.0 / E, bias=256.0 * EPS
+            )
+
+        def finish(u):
+            c, h = divmod(u, H)
+            nc.vector.scalar_tensor_tensor(
+                out=res[u][:], in0=y_of(u), scalar=rinv[:, u : u + 1], in1=gn_sb[:], op0=MULT, op1=MULT
+            )
+            nc.sync.dma_start(out=out[h, c * QC : (c + 1) * QC, :], in_=res[u][:])
+
+        copy_k(nc.vector.tensor_copy, 0, K_SPLIT)
+        copy_k(nc.scalar.copy, K_SPLIT, P)
+        for r in range(PACK):
+            quant_k(r)
+        copy_q(nc.scalar.copy, 0)
+        quant_q(0)
+        scores(0)
+        copy_q(nc.vector.tensor_copy, 1)
+        make_mt(0, 0, 1)
+        quant_q(1)
+        scores(1)
+        make_mt(0, 1, PACK)
+        act_silu(0)
+        act_silu(1)
+        weigh(0)
+        weigh(1)
+        copy_q(nc.scalar.copy, 2)
+        quant_w(0)
+        quant_q(2)
+        scores(2)
+        quant_w(1)
+        act_silu(2)
+        weigh(2)
+        copy_q(nc.scalar.copy, 3)
+        make_mt(1, 0, PACK)
+        act_silu(3)
+        quant_q(3)
+        scores(3)
+        weigh(3)
+        quant_w(2)
+        copy_v()
+        quant_w(3)
+        quant_v()
+        for u in range(4):
+            values(u)
+        for u in range(4, UNITS):
+            act_silu(u)
+        for u in range(4):
+            square(u)
+        root(0, 4)
+        weigh(4)
+        weigh(5)
+        quant_w(4)
+        weigh(6)
+        quant_w(5)
+        values(4)
+        values(5)
+        square(4)
+        square(5)
+        root(4, 6)
+        weigh(7)
+        quant_w(6)
+        values(6)
+        square(6)
+        root(6, 7)
+        finish(0)
+        quant_w(7)
+        values(7)
+        square(7)
+        root(7, 8)
+        for u in range(1, UNITS):
+            finish(u)

@@ -20,10 +20,11 @@ QC = 128
 CHUNKS = NQ // QC
 HALF = NQ // 2
 RUN = 4
-K_SPLIT = 84
+K_SPLIT = 72
 UNITS = CHUNKS * H
 Y_BANK = [(0, 0), (0, 1), (0, 2), (0, 3), (1, 0), (1, 1), (2, 0), (3, 0)]
 EPS = 1e-5
+Q_LOADS = [(0, QC), (QC, 2 * QC), (2 * QC, NQ)]
 
 
 def tile_rows_a_silu_mask_onorm_kernel(tc, qT, kT, t, v, mask, gn, out):
@@ -37,21 +38,26 @@ def tile_rows_a_silu_mask_onorm_kernel(tc, qT, kT, t, v, mask, gn, out):
             return sb.tile(shape, dtype, name=name, align_bytes=64)
 
         k_raw = sbuf("k_raw", [P, PACK, N], F32)
-        q_raw = [sbuf("q_raw%d" % a, [P, PACK, HALF], F32) for a in range(2)]
+        q_raw = [sbuf("q_raw%d" % a, [P, PACK, c1 - c0], F32) for a, (c0, c1) in enumerate(Q_LOADS)]
         m_raw = [sbuf("m_raw%d" % a, [P, PACK, HALF], F32) for a in range(2)]
         t_sb = sbuf("t_sb", [P, PACK], F32)
         v_raw = sbuf("v_raw", [P, H, PACK, E], F32)
         gn_sb = sbuf("gn_sb", [P, E], F32)
 
+        warm = sbuf("warm", [P, 2], F32)
+        nc.gpsimd.memset(warm[:, 0:1], 0.0)
+        nc.scalar.activation(out=warm[:, 1:2], in_=warm[:, 0:1], func=ACT.Silu)
+
         q_view = qT.rearrange("h (p j) q -> (h p) j q", j=PACK)
         m_view = mask.rearrange("(p r) q -> p r q", r=PACK)
         nc.sync.dma_start(out=k_raw[:], in_=kT.rearrange("h (p j) n -> (h p) j n", j=PACK))
-        nc.sync.dma_start(out=q_raw[0][:], in_=q_view[:, :, 0:HALF])
+        nc.sync.dma_start(out=q_raw[0][:], in_=q_view[:, :, 0:QC])
+        nc.sync.dma_start(out=q_raw[1][:], in_=q_view[:, :, QC:HALF])
         nc.sync.dma_start(out=t_sb[:], in_=t.rearrange("(p r) o -> p (r o)", r=PACK))
         nc.sync.dma_start(out=m_raw[0][:], in_=m_view[:, :, 0:HALF])
-        nc.sync.dma_start(out=q_raw[1][:], in_=q_view[:, :, HALF:NQ])
-        nc.sync.dma_start(out=m_raw[1][:], in_=m_view[:, :, HALF:NQ])
+        nc.sync.dma_start(out=q_raw[2][:], in_=q_view[:, :, HALF:NQ])
         nc.sync.dma_start(out=v_raw[:], in_=v.rearrange("h (p r) e -> p h r e", r=PACK))
+        nc.sync.dma_start(out=m_raw[1][:], in_=m_view[:, :, HALF:NQ])
         nc.sync.dma_start(out=gn_sb[:], in_=gn)
 
         k_bf = sbuf("k_bf", [P, PACK, P, PACK], BF16)
@@ -91,7 +97,8 @@ def tile_rows_a_silu_mask_onorm_kernel(tc, qT, kT, t, v, mask, gn, out):
             return c // 2, slice((c % 2) * QC, (c % 2 + 1) * QC)
 
         def copy_q(copy, c):
-            a, cols = half_cols(c)
+            a = min(c, 2)
+            cols = slice(c * QC - Q_LOADS[a][0], (c + 1) * QC - Q_LOADS[a][0])
             copy(
                 out=q_bf[c][:].rearrange("p (c i) j -> p c j i", i=RUN),
                 in_=q_raw[a][:, :, cols].rearrange("p j (c i) -> p c j i", i=RUN),
@@ -186,63 +193,76 @@ def tile_rows_a_silu_mask_onorm_kernel(tc, qT, kT, t, v, mask, gn, out):
 
         copy_k(nc.vector.tensor_copy, 0, K_SPLIT)
         copy_k(nc.scalar.copy, K_SPLIT, P)
-        for r in range(PACK):
-            quant_k(r)
-        copy_q(nc.scalar.copy, 0)
+        copy_q(nc.vector.tensor_copy, 0)
+        quant_k(0)
         quant_q(0)
+        quant_k(1)
+        quant_k(2)
+        quant_k(3)
         scores(0)
-        copy_q(nc.vector.tensor_copy, 1)
-        make_mt(0, 0, 1)
+        copy_q(nc.scalar.copy, 1)
         quant_q(1)
         scores(1)
-        make_mt(0, 1, PACK)
+        make_mt(0, 0, 4)
         act_silu(0)
         act_silu(1)
         weigh(0)
-        weigh(1)
         copy_q(nc.scalar.copy, 2)
-        quant_w(0)
+        weigh(1)
         quant_q(2)
         scores(2)
-        quant_w(1)
+        quant_w(0)
         act_silu(2)
-        weigh(2)
         copy_q(nc.scalar.copy, 3)
-        make_mt(1, 0, PACK)
         act_silu(3)
+        copy_v()
+        quant_w(1)
         quant_q(3)
         scores(3)
+        weigh(2)
+        quant_v()
+        values(0)
+        values(1)
         weigh(3)
         quant_w(2)
-        copy_v()
+        make_mt(1, 0, 4)
         quant_w(3)
-        quant_v()
-        for u in range(4):
-            values(u)
-        for u in range(4, UNITS):
-            act_silu(u)
-        for u in range(4):
-            square(u)
-        root(0, 4)
+        act_silu(4)
+        act_silu(5)
+        act_silu(6)
+        square(0)
+        square(1)
+        act_silu(7)
+        root(0, 2)
+        values(2)
+        values(3)
+        square(2)
+        square(3)
+        root(2, 4)
         weigh(4)
         weigh(5)
         quant_w(4)
+        values(4)
         weigh(6)
         quant_w(5)
-        values(4)
         values(5)
         square(4)
         square(5)
-        root(4, 6)
         weigh(7)
         quant_w(6)
         values(6)
-        square(6)
-        root(6, 7)
         finish(0)
         quant_w(7)
         values(7)
+        root(4, 6)
+        square(6)
         square(7)
+        root(6, 7)
         root(7, 8)
-        for u in range(1, UNITS):
-            finish(u)
+        finish(1)
+        finish(2)
+        finish(3)
+        finish(4)
+        finish(5)
+        finish(6)
+        finish(7)

@@ -19,7 +19,7 @@ ROWS = D // PACK
 QC = 128
 CHUNKS = NQ // QC
 HALF = NQ // 2
-RUN = 4
+RUN = 2
 K_SPLIT = 72
 UNITS = CHUNKS * H
 Y_BANK = [(0, 0), (0, 1), (0, 2), (0, 3), (1, 0), (1, 1), (2, 0), (3, 0)]

@@ -4,6 +4,8 @@ import concourse.mybir as mybir
 
 H, D, NQ, N, E = 2, 256, 512, 512, 128
 FLOPS = 2 * H * N * NQ * (D + E)
+EPS = 1e-5
+Y_DIV = 16.0
 
 F32 = mybir.dt.float32
 BF16 = mybir.dt.bfloat16
@@ -18,13 +20,12 @@ PACK = 4
 ROWS = D // PACK
 QC = 128
 CHUNKS = NQ // QC
+UNITS = CHUNKS * H
 HALF = NQ // 2
 RUN = 2
 K_SPLIT = 72
-UNITS = CHUNKS * H
-Y_BANK = [(0, 0), (0, 1), (0, 2), (0, 3), (1, 0), (1, 1), (2, 0), (3, 0)]
-EPS = 1e-5
 Q_LOADS = [(0, QC), (QC, 2 * QC), (2 * QC, NQ)]
+Y_BANK = [(0, 0), (0, 1), (0, 2), (0, 3), (1, 0), (1, 1), (2, 0), (3, 0)]
 
 
 def tile_rows_a_silu_mask_onorm_kernel(tc, qT, kT, t, v, mask, gn, out):
@@ -44,6 +45,8 @@ def tile_rows_a_silu_mask_onorm_kernel(tc, qT, kT, t, v, mask, gn, out):
         v_raw = sbuf("v_raw", [P, H, PACK, E], F32)
         gn_sb = sbuf("gn_sb", [P, E], F32)
 
+        nc.scalar.dma_start(out=t_sb[:], in_=t.rearrange("(p r) o -> p (r o)", r=PACK))
+
         warm = sbuf("warm", [P, 2], F32)
         nc.gpsimd.memset(warm[:, 0:1], 0.0)
         nc.scalar.activation(out=warm[:, 1:2], in_=warm[:, 0:1], func=ACT.Silu)
@@ -53,7 +56,6 @@ def tile_rows_a_silu_mask_onorm_kernel(tc, qT, kT, t, v, mask, gn, out):
         nc.sync.dma_start(out=k_raw[:], in_=kT.rearrange("h (p j) n -> (h p) j n", j=PACK))
         nc.sync.dma_start(out=q_raw[0][:], in_=q_view[:, :, 0:QC])
         nc.sync.dma_start(out=q_raw[1][:], in_=q_view[:, :, QC:HALF])
-        nc.sync.dma_start(out=t_sb[:], in_=t.rearrange("(p r) o -> p (r o)", r=PACK))
         nc.sync.dma_start(out=m_raw[0][:], in_=m_view[:, :, 0:HALF])
         nc.sync.dma_start(out=q_raw[2][:], in_=q_view[:, :, HALF:NQ])
         nc.sync.dma_start(out=v_raw[:], in_=v.rearrange("h (p r) e -> p h r e", r=PACK))
@@ -93,15 +95,12 @@ def tile_rows_a_silu_mask_onorm_kernel(tc, qT, kT, t, v, mask, gn, out):
         def quant_k(r):
             quantize(k_codes[:, r, :], k_scales[:, r, :], k_bf[:, r, :, :].rearrange("p s j -> p (s j)"))
 
-        def half_cols(c):
-            return c // 2, slice((c % 2) * QC, (c % 2 + 1) * QC)
-
         def copy_q(copy, c):
-            a = min(c, 2)
+            a = min(c, len(Q_LOADS) - 1)
             cols = slice(c * QC - Q_LOADS[a][0], (c + 1) * QC - Q_LOADS[a][0])
             copy(
-                out=q_bf[c][:].rearrange("p (c i) j -> p c j i", i=RUN),
-                in_=q_raw[a][:, :, cols].rearrange("p j (c i) -> p c j i", i=RUN),
+                out=q_bf[c][:].rearrange("p (g i) j -> p g j i", i=RUN),
+                in_=q_raw[a][:, :, cols].rearrange("p j (g i) -> p g j i", i=RUN),
             )
 
         def quant_q(c):
@@ -109,8 +108,8 @@ def tile_rows_a_silu_mask_onorm_kernel(tc, qT, kT, t, v, mask, gn, out):
 
         def copy_v():
             nc.vector.tensor_copy(
-                out=v_bf[:].rearrange("p h (c i) r -> p h c r i", i=RUN),
-                in_=v_raw[:].rearrange("p h r (c i) -> p h c r i", i=RUN),
+                out=v_bf[:].rearrange("p h (g i) r -> p h g r i", i=RUN),
+                in_=v_raw[:].rearrange("p h r (g i) -> p h g r i", i=RUN),
             )
 
         def quant_v():
@@ -120,16 +119,16 @@ def tile_rows_a_silu_mask_onorm_kernel(tc, qT, kT, t, v, mask, gn, out):
                 v_bf[:].rearrange("p h e r -> p (h e r)"),
             )
 
-        def make_mt(a, r0, r1):
-            for r in range(r0, r1):
+        def make_mt(a):
+            for r in range(PACK):
                 nc.vector.tensor_scalar(
                     out=mt[a][:, r, :], in0=m_raw[a][:, r, :], scalar1=t_sb[:, r : r + 1], scalar2=None, op0=MULT
                 )
 
         def scores(c):
             for h in range(H):
+                rows = slice(h * ROWS, (h + 1) * ROWS)
                 for r in range(PACK):
-                    rows = slice(h * ROWS, (h + 1) * ROWS)
                     nc.tensor.matmul_mx(
                         out=s_banks[h][c % 2][:, r, :],
                         lhsT=k_codes[rows, r, :].bitcast(FP8X4),
@@ -143,17 +142,17 @@ def tile_rows_a_silu_mask_onorm_kernel(tc, qT, kT, t, v, mask, gn, out):
         def act_silu(u):
             c, h = divmod(u, H)
             nc.scalar.activation(
-                out=silu[u][:].rearrange("p (c r i) -> p c r i", r=PACK, i=RUN),
-                in_=s_banks[h][c % 2][:].rearrange("p r (c i) -> p c r i", i=RUN),
+                out=silu[u][:].rearrange("p (g r i) -> p g r i", r=PACK, i=RUN),
+                in_=s_banks[h][c % 2][:].rearrange("p r (g i) -> p g r i", i=RUN),
                 func=ACT.Silu,
             )
 
         def weigh(u):
-            a, cols = half_cols(u // H)
+            a, b = divmod(u // H, 2)
             nc.vector.tensor_tensor(
-                out=w_bf[u][:].rearrange("p (c i) r -> p c r i", i=RUN),
-                in0=silu[u][:].rearrange("p (c r i) -> p c r i", r=PACK, i=RUN),
-                in1=mt[a][:, :, cols].rearrange("p r (c i) -> p c r i", i=RUN),
+                out=w_bf[u][:].rearrange("p (g i) r -> p g r i", i=RUN),
+                in0=silu[u][:].rearrange("p (g r i) -> p g r i", r=PACK, i=RUN),
+                in1=mt[a][:, :, b * QC : (b + 1) * QC].rearrange("p r (g i) -> p g r i", i=RUN),
                 op=MULT,
             )
 
@@ -161,8 +160,8 @@ def tile_rows_a_silu_mask_onorm_kernel(tc, qT, kT, t, v, mask, gn, out):
             quantize(w_codes[u][:], w_scales[u][:], w_bf[u][:].rearrange("p q r -> p (q r)"))
 
         def y_of(u):
-            b, s = Y_BANK[u]
-            return y_banks[b][:, s, :]
+            bank, slot = Y_BANK[u]
+            return y_banks[bank][:, slot, :]
 
         def values(u):
             h = u % H
@@ -181,7 +180,11 @@ def tile_rows_a_silu_mask_onorm_kernel(tc, qT, kT, t, v, mask, gn, out):
 
         def root(u0, u1):
             nc.scalar.activation(
-                out=rinv[:, u0:u1], in_=sums[:, u0:u1], func=ACT.Abs_reciprocal_sqrt, scale=1.0 / E, bias=256.0 * EPS
+                out=rinv[:, u0:u1],
+                in_=sums[:, u0:u1],
+                func=ACT.Abs_reciprocal_sqrt,
+                scale=1.0 / E,
+                bias=Y_DIV * Y_DIV * EPS,
             )
 
         def finish(u):
@@ -191,19 +194,20 @@ def tile_rows_a_silu_mask_onorm_kernel(tc, qT, kT, t, v, mask, gn, out):
             )
             nc.sync.dma_start(out=out[h, c * QC : (c + 1) * QC, :], in_=res[u][:])
 
+
         copy_k(nc.vector.tensor_copy, 0, K_SPLIT)
         copy_k(nc.scalar.copy, K_SPLIT, P)
         copy_q(nc.vector.tensor_copy, 0)
         quant_k(0)
         quant_q(0)
-        quant_k(1)
-        quant_k(2)
-        quant_k(3)
+        for r in range(1, PACK):
+            quant_k(r)
         scores(0)
         copy_q(nc.scalar.copy, 1)
         quant_q(1)
         scores(1)
-        make_mt(0, 0, 4)
+        make_mt(0)
+
         act_silu(0)
         act_silu(1)
         weigh(0)
@@ -225,20 +229,21 @@ def tile_rows_a_silu_mask_onorm_kernel(tc, qT, kT, t, v, mask, gn, out):
         values(1)
         weigh(3)
         quant_w(2)
-        make_mt(1, 0, 4)
+        make_mt(1)
         quant_w(3)
-        act_silu(4)
-        act_silu(5)
-        act_silu(6)
+
+        for u in range(4, UNITS - 1):
+            act_silu(u)
         square(0)
         square(1)
-        act_silu(7)
+        act_silu(UNITS - 1)
         root(0, 2)
         values(2)
         values(3)
         square(2)
         square(3)
         root(2, 4)
+
         weigh(4)
         weigh(5)
         quant_w(4)
@@ -259,10 +264,6 @@ def tile_rows_a_silu_mask_onorm_kernel(tc, qT, kT, t, v, mask, gn, out):
         square(7)
         root(6, 7)
         root(7, 8)
-        finish(1)
-        finish(2)
-        finish(3)
-        finish(4)
-        finish(5)
-        finish(6)
-        finish(7)
+
+        for u in range(1, UNITS):
+            finish(u)

from contextlib import ExitStack

import concourse.mybir as mybir

H, D, NQ, N, E = 2, 256, 512, 512, 128
FLOPS = 2 * H * N * NQ * (D + E)
EPS = 1e-5
Y_DIV = 16.0

F32 = mybir.dt.float32
BF16 = mybir.dt.bfloat16
U32 = mybir.dt.uint32
U8 = mybir.dt.uint8
FP8X4 = mybir.dt.float8_e4m3fn_x4
ACT = mybir.ActivationFunctionType
MULT = mybir.AluOpType.mult

P = 128
PACK = 4
ROWS = D // PACK
QC = 128
CHUNKS = NQ // QC
UNITS = CHUNKS * H
HALF = NQ // 2
RUN = 2
K_SPLIT = 72
Q_LOADS = [(0, QC), (QC, 2 * QC), (2 * QC, NQ)]
Y_BANK = [(0, 0), (0, 1), (0, 2), (0, 3), (1, 0), (1, 1), (2, 0), (3, 0)]


def tile_rows_a_silu_mask_onorm_kernel(tc, qT, kT, t, v, mask, gn, out):
    nc = tc.nc
    with ExitStack() as ctx:
        sb = ctx.enter_context(tc.tile_pool(name="sb", bufs=1))
        ps = ctx.enter_context(tc.psum_pool(name="ps", bufs=1))
        ctx.enter_context(tc.manual_schedule())

        def sbuf(name, shape, dtype):
            return sb.tile(shape, dtype, name=name, align_bytes=64)

        k_raw = sbuf("k_raw", [P, PACK, N], F32)
        q_raw = [sbuf("q_raw%d" % a, [P, PACK, c1 - c0], F32) for a, (c0, c1) in enumerate(Q_LOADS)]
        m_raw = [sbuf("m_raw%d" % a, [P, PACK, HALF], F32) for a in range(2)]
        t_sb = sbuf("t_sb", [P, PACK], F32)
        v_raw = sbuf("v_raw", [P, H, PACK, E], F32)
        gn_sb = sbuf("gn_sb", [P, E], F32)

        nc.scalar.dma_start(out=t_sb[:], in_=t.rearrange("(p r) o -> p (r o)", r=PACK))

        warm = sbuf("warm", [P, 2], F32)
        nc.gpsimd.memset(warm[:, 0:1], 0.0)
        nc.scalar.activation(out=warm[:, 1:2], in_=warm[:, 0:1], func=ACT.Silu)

        q_view = qT.rearrange("h (p j) q -> (h p) j q", j=PACK)
        m_view = mask.rearrange("(p r) q -> p r q", r=PACK)
        nc.sync.dma_start(out=k_raw[:], in_=kT.rearrange("h (p j) n -> (h p) j n", j=PACK))
        nc.sync.dma_start(out=q_raw[0][:], in_=q_view[:, :, 0:QC])
        nc.sync.dma_start(out=q_raw[1][:], in_=q_view[:, :, QC:HALF])
        nc.sync.dma_start(out=m_raw[0][:], in_=m_view[:, :, 0:HALF])
        nc.sync.dma_start(out=q_raw[2][:], in_=q_view[:, :, HALF:NQ])
        nc.sync.dma_start(out=v_raw[:], in_=v.rearrange("h (p r) e -> p h r e", r=PACK))
        nc.sync.dma_start(out=m_raw[1][:], in_=m_view[:, :, HALF:NQ])
        nc.sync.dma_start(out=gn_sb[:], in_=gn)

        k_bf = sbuf("k_bf", [P, PACK, P, PACK], BF16)
        k_codes = sbuf("k_codes", [P, PACK, P], U32)
        k_scales = sbuf("k_scales", [P, PACK, P], U8)
        q_bf = [sbuf("q_bf%d" % c, [P, QC, PACK], BF16) for c in range(CHUNKS)]
        q_codes = [sbuf("q_codes%d" % c, [P, QC], U32) for c in range(CHUNKS)]
        q_scales = [sbuf("q_scales%d" % c, [P, QC], U8) for c in range(CHUNKS)]
        v_bf = sbuf("v_bf", [P, H, E, PACK], BF16)
        v_codes = sbuf("v_codes", [P, H, E], U32)
        v_scales = sbuf("v_scales", [P, H, E], U8)
        mt = [sbuf("mt%d" % a, [P, PACK, HALF], F32) for a in range(2)]
        silu = [sbuf("silu%d" % u, [P, PACK * QC], F32) for u in range(UNITS)]
        w_bf = [sbuf("w_bf%d" % u, [P, QC, PACK], BF16) for u in range(UNITS)]
        w_codes = [sbuf("w_codes%d" % u, [P, QC], U32) for u in range(UNITS)]
        w_scales = [sbuf("w_scales%d" % u, [P, QC], U8) for u in range(UNITS)]
        squares = [sbuf("squares%d" % u, [P, E], BF16) for u in range(UNITS)]
        sums = sbuf("sums", [P, UNITS], F32)
        rinv = sbuf("rinv", [P, UNITS], F32)
        res = [sbuf("res%d" % u, [P, E], F32) for u in range(UNITS)]
        s_banks = [[ps.tile([P, PACK, QC], F32, name="s%d_%d" % (h, b)) for b in range(2)] for h in range(H)]
        y_banks = [ps.tile([P, PACK, E], F32, name="y%d" % b) for b in range(4)]

        def quantize(codes, scales, src):
            nc.vector.quantize_mx(out=codes.bitcast(FP8X4), scales=scales, in_=src)

        def copy_k(copy, s0, s1):
            copy(
                out=k_bf[:, :, s0:s1, :].rearrange("p r s j -> p s j r"),
                in_=k_raw[:, :, PACK * s0 : PACK * s1].rearrange("p j (s r) -> p s j r", r=PACK),
            )

        def quant_k(r):
            quantize(k_codes[:, r, :], k_scales[:, r, :], k_bf[:, r, :, :].rearrange("p s j -> p (s j)"))

        def copy_q(copy, c):
            a = min(c, len(Q_LOADS) - 1)
            cols = slice(c * QC - Q_LOADS[a][0], (c + 1) * QC - Q_LOADS[a][0])
            copy(
                out=q_bf[c][:].rearrange("p (g i) j -> p g j i", i=RUN),
                in_=q_raw[a][:, :, cols].rearrange("p j (g i) -> p g j i", i=RUN),
            )

        def quant_q(c):
            quantize(q_codes[c][:], q_scales[c][:], q_bf[c][:].rearrange("p q j -> p (q j)"))

        def copy_v():
            nc.vector.tensor_copy(
                out=v_bf[:].rearrange("p h (g i) r -> p h g r i", i=RUN),
                in_=v_raw[:].rearrange("p h r (g i) -> p h g r i", i=RUN),
            )

        def quant_v():
            quantize(
                v_codes[:].rearrange("p h e -> p (h e)"),
                v_scales[:].rearrange("p h e -> p (h e)"),
                v_bf[:].rearrange("p h e r -> p (h e r)"),
            )

        def make_mt(a):
            for r in range(PACK):
                nc.vector.tensor_scalar(
                    out=mt[a][:, r, :], in0=m_raw[a][:, r, :], scalar1=t_sb[:, r : r + 1], scalar2=None, op0=MULT
                )

        def scores(c):
            for h in range(H):
                rows = slice(h * ROWS, (h + 1) * ROWS)
                for r in range(PACK):
                    nc.tensor.matmul_mx(
                        out=s_banks[h][c % 2][:, r, :],
                        lhsT=k_codes[rows, r, :].bitcast(FP8X4),
                        lhsT_scale=k_scales[rows, r, :],
                        rhs=q_codes[c][rows, :].bitcast(FP8X4),
                        rhs_scale=q_scales[c][rows, :],
                        start=True,
                        stop=True,
                    )

        def act_silu(u):
            c, h = divmod(u, H)
            nc.scalar.activation(
                out=silu[u][:].rearrange("p (g r i) -> p g r i", r=PACK, i=RUN),
                in_=s_banks[h][c % 2][:].rearrange("p r (g i) -> p g r i", i=RUN),
                func=ACT.Silu,
            )

        def weigh(u):
            a, b = divmod(u // H, 2)
            nc.vector.tensor_tensor(
                out=w_bf[u][:].rearrange("p (g i) r -> p g r i", i=RUN),
                in0=silu[u][:].rearrange("p (g r i) -> p g r i", r=PACK, i=RUN),
                in1=mt[a][:, :, b * QC : (b + 1) * QC].rearrange("p r (g i) -> p g r i", i=RUN),
                op=MULT,
            )

        def quant_w(u):
            quantize(w_codes[u][:], w_scales[u][:], w_bf[u][:].rearrange("p q r -> p (q r)"))

        def y_of(u):
            bank, slot = Y_BANK[u]
            return y_banks[bank][:, slot, :]

        def values(u):
            h = u % H
            nc.tensor.matmul_mx(
                out=y_of(u),
                lhsT=w_codes[u][:].bitcast(FP8X4),
                lhsT_scale=w_scales[u][:],
                rhs=v_codes[:, h, :].bitcast(FP8X4),
                rhs_scale=v_scales[:, h, :],
                start=True,
                stop=True,
            )

        def square(u):
            nc.scalar.activation(out=squares[u][:], in_=y_of(u), func=ACT.Square, accum_out=sums[:, u : u + 1])

        def root(u0, u1):
            nc.scalar.activation(
                out=rinv[:, u0:u1],
                in_=sums[:, u0:u1],
                func=ACT.Abs_reciprocal_sqrt,
                scale=1.0 / E,
                bias=Y_DIV * Y_DIV * EPS,
            )

        def finish(u):
            c, h = divmod(u, H)
            nc.vector.scalar_tensor_tensor(
                out=res[u][:], in0=y_of(u), scalar=rinv[:, u : u + 1], in1=gn_sb[:], op0=MULT, op1=MULT
            )
            nc.sync.dma_start(out=out[h, c * QC : (c + 1) * QC, :], in_=res[u][:])


        copy_k(nc.vector.tensor_copy, 0, K_SPLIT)
        copy_k(nc.scalar.copy, K_SPLIT, P)
        copy_q(nc.vector.tensor_copy, 0)
        quant_k(0)
        quant_q(0)
        for r in range(1, PACK):
            quant_k(r)
        scores(0)
        copy_q(nc.scalar.copy, 1)
        quant_q(1)
        scores(1)
        make_mt(0)

        act_silu(0)
        act_silu(1)
        weigh(0)
        copy_q(nc.scalar.copy, 2)
        weigh(1)
        quant_q(2)
        scores(2)
        quant_w(0)
        act_silu(2)
        copy_q(nc.scalar.copy, 3)
        act_silu(3)
        copy_v()
        quant_w(1)
        quant_q(3)
        scores(3)
        weigh(2)
        quant_v()
        values(0)
        values(1)
        weigh(3)
        quant_w(2)
        make_mt(1)
        quant_w(3)

        for u in range(4, UNITS - 1):
            act_silu(u)
        square(0)
        square(1)
        act_silu(UNITS - 1)
        root(0, 2)
        values(2)
        values(3)
        square(2)
        square(3)
        root(2, 4)

        weigh(4)
        weigh(5)
        quant_w(4)
        values(4)
        weigh(6)
        quant_w(5)
        values(5)
        square(4)
        square(5)
        weigh(7)
        quant_w(6)
        values(6)
        finish(0)
        quant_w(7)
        values(7)
        root(4, 6)
        square(6)
        square(7)
        root(6, 7)
        root(7, 8)

        for u in range(1, UNITS):
            finish(u)
